import numpy as np
import ml_dtypes

BF16 = ml_dtypes.bfloat16


def bf(x):
    return np.asarray(x, np.float32).astype(BF16)


def f32(x):
    return np.asarray(x, np.float32)


def f64(x):
    return np.asarray(x).astype(np.float64)


def striped(idx):
    return np.tile(idx.reshape(-1, 16).T, (8, 1))


S, K, M, N, D, V = 2048, 256, 256, 768, 3, 256


def gelu_tanh(v):
    return 0.5 * v * (1.0 + np.tanh(np.sqrt(2.0 / np.pi) * (v + 0.044715 * v**3)))


def setup_inputs():
    return {"table": bf(np.random.standard_normal((K, S))), "w": bf(np.random.standard_normal((D, K, M)) / np.sqrt(D * K)), "b": f32(0.5 * np.random.standard_normal((M, 1))), "offs": striped(np.random.permutation(np.tile(np.arange(S), 2))[:N])}


def reference(table, w, b, offs):
    idx = offs[:16].T.reshape(-1)
    x = f64(table)[:, idx]
    y = sum(f64(w)[t].T @ x[:, t * V : (t + 1) * V] for t in range(D))
    return gelu_tanh(y + f64(b))

@@ -1,0 +1,57 @@
+import concourse.mybir as mybir
+
+BF16, F32, U16 = mybir.dt.bfloat16, mybir.dt.float32, mybir.dt.uint16
+GELU_TANH = mybir.ActivationFunctionType.Gelu_apprx_tanh
+
+P = 128
+RELATIONS = 3
+NODES = 256
+K, M, S = 256, 256, 2048
+OFFSETS = NODES // 16
+
+FLOPS = 2 * RELATIONS * NODES * K * M
+
+
+def tile_gather_matmul_kernel(tc, table, w, b, offs, out):
+    nc = tc.nc
+    with (
+        tc.tile_pool(name="held", bufs=1) as held,
+        tc.psum_pool(name="psum", bufs=1) as psum,
+    ):
+        offsets = held.tile([P, RELATIONS * OFFSETS], U16, name="offsets")
+        blocks = [held.tile([P, S], BF16, name=f"table{c}") for c in range(K // P)]
+        weights = [held.tile([P, RELATIONS, M], BF16, name=f"weights{c}") for c in range(K // P)]
+        bias = held.tile([P, M // P], F32, name="bias")
+
+        def load_weights(queue, c):
+            queue.dma_start(weights[c][:], w[:, c * P : (c + 1) * P, :].rearrange("t p m -> p t m"))
+
+        nc.sync.dma_start(offsets[:], offs)
+        load_weights(nc.scalar, 0)
+        nc.sync.dma_start(blocks[0][:], table[0:P, :])
+        load_weights(nc.sync, 1)
+        nc.sync.dma_start(blocks[1][:], table[P : 2 * P, :])
+        nc.scalar.dma_start(bias[:], b.rearrange("(a p) o -> p (a o)", p=P))
+
+        zero = held.tile([P, 1], F32, name="zero")
+        unread = held.tile([P, 1], F32, name="unread")
+        nc.vector.memset(zero[:], 0.0)
+        nc.scalar.activation(unread[:], zero[:], GELU_TANH)
+
+        banks = [psum.tile([P, NODES], F32, name=f"bank{a}") for a in range(M // P)]
+        for c in range(K // P):
+            for a in range(M // P):
+                for t in range(RELATIONS):
+                    picked = blocks[c][:].indirect(offsets[:, t * OFFSETS : (t + 1) * OFFSETS])
+                    nc.tensor.matmul(
+                        banks[a][:],
+                        weights[c][:, t, a * P : (a + 1) * P],
+                        picked,
+                        start=(c == 0 and t == 0),
+                        stop=(c == K // P - 1 and t == RELATIONS - 1),
+                    )
+
+        for a in range(M // P):
+            activated = held.tile([P, NODES], F32, name=f"activated{a}")
+            nc.scalar.activation(activated[:], banks[a][:], GELU_TANH, bias=bias[:, a : a + 1])
+            nc.sync.dma_start(out[a * P : (a + 1) * P, :], activated[:])

@@ -7,6 +7,7 @@ P = 128
 RELATIONS = 3
 NODES = 256
 K, M, S = 256, 256, 2048
+BLOCKS = K // P
 OFFSETS = NODES // 16
 
 FLOPS = 2 * RELATIONS * NODES * K * M
@@ -19,18 +20,19 @@ def tile_gather_matmul_kernel(tc, table, w, b, offs, out):
         tc.psum_pool(name="psum", bufs=1) as psum,
     ):
         offsets = held.tile([P, RELATIONS * OFFSETS], U16, name="offsets")
-        blocks = [held.tile([P, S], BF16, name=f"table{c}") for c in range(K // P)]
-        weights = [held.tile([P, RELATIONS, M], BF16, name=f"weights{c}") for c in range(K // P)]
+        blocks = [held.tile([P, S], BF16, name=f"table{c}") for c in range(BLOCKS)]
+        weights_first = held.tile([P, 1, BLOCKS, M], BF16, name="weights_first")
+        weights_rest = held.tile([P, RELATIONS - 1, BLOCKS, M], BF16, name="weights_rest")
         bias = held.tile([P, M // P], F32, name="bias")
 
-        def load_weights(queue, c):
-            queue.dma_start(weights[c][:], w[:, c * P : (c + 1) * P, :].rearrange("t p m -> p t m"))
+        table_blocks = table.rearrange("(p c) s -> c p s", c=BLOCKS)
+        w_rows = w.rearrange("t (p c) m -> p t c m", c=BLOCKS)
 
         nc.sync.dma_start(offsets[:], offs)
-        load_weights(nc.scalar, 0)
-        nc.sync.dma_start(blocks[0][:], table[0:P, :])
-        load_weights(nc.sync, 1)
-        nc.sync.dma_start(blocks[1][:], table[P : 2 * P, :])
+        nc.scalar.dma_start(weights_first[:], w_rows[:, 0:1])
+        nc.sync.dma_start(blocks[0][:], table_blocks[0])
+        nc.sync.dma_start(weights_rest[:], w_rows[:, 1:RELATIONS])
+        nc.sync.dma_start(blocks[1][:], table_blocks[1])
         nc.scalar.dma_start(bias[:], b.rearrange("(a p) o -> p (a o)", p=P))
 
         zero = held.tile([P, 1], F32, name="zero")
@@ -39,17 +41,23 @@ def tile_gather_matmul_kernel(tc, table, w, b, offs, out):
         nc.scalar.activation(unread[:], zero[:], GELU_TANH)
 
         banks = [psum.tile([P, NODES], F32, name=f"bank{a}") for a in range(M // P)]
-        for c in range(K // P):
+
+        def add_product(a, c, t):
+            weights = weights_first[:, 0, c] if t == 0 else weights_rest[:, t - 1, c]
+            nc.tensor.matmul(
+                banks[a][:],
+                weights[:, a * P : (a + 1) * P],
+                blocks[c][:].indirect(offsets[:, t * OFFSETS : (t + 1) * OFFSETS]),
+                start=(c == 0 and t == 0),
+                stop=(c == BLOCKS - 1 and t == RELATIONS - 1),
+            )
+
+        for t in range(RELATIONS):
             for a in range(M // P):
-                for t in range(RELATIONS):
-                    picked = blocks[c][:].indirect(offsets[:, t * OFFSETS : (t + 1) * OFFSETS])
-                    nc.tensor.matmul(
-                        banks[a][:],
-                        weights[c][:, t, a * P : (a + 1) * P],
-                        picked,
-                        start=(c == 0 and t == 0),
-                        stop=(c == K // P - 1 and t == RELATIONS - 1),
-                    )
+                add_product(a, 0, t)
+        for a in range(M // P):
+            for t in range(RELATIONS):
+                add_product(a, 1, t)
 
         for a in range(M // P):
             activated = held.tile([P, NODES], F32, name=f"activated{a}")

@@ -28,12 +28,12 @@ def tile_gather_matmul_kernel(tc, table, w, b, offs, out):
         table_blocks = table.rearrange("(p c) s -> c p s", c=BLOCKS)
         w_rows = w.rearrange("t (p c) m -> p t c m", c=BLOCKS)
 
-        nc.sync.dma_start(offsets[:], offs)
-        nc.scalar.dma_start(weights_first[:], w_rows[:, 0:1])
         nc.sync.dma_start(blocks[0][:], table_blocks[0])
+        nc.scalar.dma_start(weights_first[:], w_rows[:, 0:1])
+        nc.sync.dma_start(offsets[:], offs)
         nc.sync.dma_start(weights_rest[:], w_rows[:, 1:RELATIONS])
         nc.sync.dma_start(blocks[1][:], table_blocks[1])
-        nc.scalar.dma_start(bias[:], b.rearrange("(a p) o -> p (a o)", p=P))
+        nc.sync.dma_start(bias[:], b.rearrange("(a p) o -> p (a o)", p=P))
 
         zero = held.tile([P, 1], F32, name="zero")
         unread = held.tile([P, 1], F32, name="unread")

import concourse.mybir as mybir

BF16, F32, U16 = mybir.dt.bfloat16, mybir.dt.float32, mybir.dt.uint16
GELU_TANH = mybir.ActivationFunctionType.Gelu_apprx_tanh

P = 128
RELATIONS = 3
NODES = 256
K, M, S = 256, 256, 2048
BLOCKS = K // P
OFFSETS = NODES // 16

FLOPS = 2 * RELATIONS * NODES * K * M


def tile_gather_matmul_kernel(tc, table, w, b, offs, out):
    nc = tc.nc
    with (
        tc.tile_pool(name="held", bufs=1) as held,
        tc.psum_pool(name="psum", bufs=1) as psum,
    ):
        offsets = held.tile([P, RELATIONS * OFFSETS], U16, name="offsets")
        blocks = [held.tile([P, S], BF16, name=f"table{c}") for c in range(BLOCKS)]
        weights_first = held.tile([P, 1, BLOCKS, M], BF16, name="weights_first")
        weights_rest = held.tile([P, RELATIONS - 1, BLOCKS, M], BF16, name="weights_rest")
        bias = held.tile([P, M // P], F32, name="bias")

        table_blocks = table.rearrange("(p c) s -> c p s", c=BLOCKS)
        w_rows = w.rearrange("t (p c) m -> p t c m", c=BLOCKS)

        nc.sync.dma_start(blocks[0][:], table_blocks[0])
        nc.scalar.dma_start(weights_first[:], w_rows[:, 0:1])
        nc.sync.dma_start(offsets[:], offs)
        nc.sync.dma_start(weights_rest[:], w_rows[:, 1:RELATIONS])
        nc.sync.dma_start(blocks[1][:], table_blocks[1])
        nc.sync.dma_start(bias[:], b.rearrange("(a p) o -> p (a o)", p=P))

        zero = held.tile([P, 1], F32, name="zero")
        unread = held.tile([P, 1], F32, name="unread")
        nc.vector.memset(zero[:], 0.0)
        nc.scalar.activation(unread[:], zero[:], GELU_TANH)

        banks = [psum.tile([P, NODES], F32, name=f"bank{a}") for a in range(M // P)]

        def add_product(a, c, t):
            weights = weights_first[:, 0, c] if t == 0 else weights_rest[:, t - 1, c]
            nc.tensor.matmul(
                banks[a][:],
                weights[:, a * P : (a + 1) * P],
                blocks[c][:].indirect(offsets[:, t * OFFSETS : (t + 1) * OFFSETS]),
                start=(c == 0 and t == 0),
                stop=(c == BLOCKS - 1 and t == RELATIONS - 1),
            )

        for t in range(RELATIONS):
            for a in range(M // P):
                add_product(a, 0, t)
        for a in range(M // P):
            for t in range(RELATIONS):
                add_product(a, 1, t)

        for a in range(M // P):
            activated = held.tile([P, NODES], F32, name=f"activated{a}")
            nc.scalar.activation(activated[:], banks[a][:], GELU_TANH, bias=bias[:, a : a + 1])
            nc.sync.dma_start(out[a * P : (a + 1) * P, :], activated[:])
